import numpy as np
import ml_dtypes


def mxq(x, axis, fmt="e4m3"):
    dtype, down = {"e4m3": (ml_dtypes.float8_e4m3fn, 7), "e5m2": (ml_dtypes.float8_e5m2, 14)}[fmt]
    v = np.moveaxis(np.asarray(x, np.float32).astype(ml_dtypes.bfloat16).astype(np.float64), axis, -1)
    blocks = v.reshape(v.shape[:-1] + (-1, 32))
    amax = np.abs(blocks).max(-1, keepdims=True)
    byte = np.maximum(np.where(amax > 0, np.frexp(amax)[1] - 1 + 127, 0) - down, 1)
    scale = np.exp2(byte - 127.0)
    codes = (blocks / scale).astype(np.float32).astype(dtype).astype(np.float64)
    return np.moveaxis((codes * scale).reshape(v.shape), -1, axis)


WIDE = False


def mx_kscale(k):
    if not WIDE:
        return np.ones(k)
    levels = np.array([30, -30])
    if k % 512:
        return np.exp2(np.random.permutation(np.resize(levels, k // 32))).repeat(32)
    a = np.empty((k // 512, 16))
    for p in range(k // 512):
        a[p, :8] = np.random.permutation(np.resize(levels, 8))
        for g in range(8):
            far = levels[np.abs(levels - a[p, g]) >= 10]
            a[p, g + 8] = far[np.random.randint(len(far))]
    return np.exp2(a.ravel()).repeat(32)


BF16 = ml_dtypes.bfloat16


def bf(x):
    return np.asarray(x, np.float32).astype(BF16)


def f64(x):
    return np.asarray(x).astype(np.float64)


E2M1 = np.array([0.0, 0.5, 1.0, 1.5, 2.0, 3.0, 4.0, 6.0, -0.0, -0.5, -1.0, -1.5, -2.0, -3.0, -4.0, -6.0])


def pack_weight(w, fmt):
    k, n = w.shape
    w = f64(bf(w)).reshape(k // 32, 32, n)
    amax = np.abs(w).max(1)
    if fmt in ("e4m3", "e5m2"):
        byte = np.frexp(amax)[1] - 1 + 127 - (7 if fmt == "e4m3" else 14)
    else:
        mant, ex = np.frexp(amax / 6.0)
        byte = np.where(mant > 0.5, ex, ex - 1) + 127
    byte = np.clip(np.where(amax > 0, byte, 1), 1, 254)
    scaled = (w * np.exp2(127.0 - byte)[:, None, :]).reshape(k, n).astype(np.float32)
    by_word = np.ascontiguousarray(scaled.reshape(k // 512, 128, 4, n).transpose(0, 1, 3, 2))
    if fmt in ("e4m3", "e5m2"):
        words = by_word.astype(ml_dtypes.float8_e4m3fn if fmt == "e4m3" else ml_dtypes.float8_e5m2).view(np.uint8)
    else:
        c = by_word.astype(ml_dtypes.float4_e2m1fn).view(np.uint8) & 0xF
        words = c[..., 0::2] | (c[..., 1::2] << 4)
    return np.ascontiguousarray(words), np.ascontiguousarray(byte.astype(np.uint8).reshape(k // 512, 16, n))


def unpack_weight(words, scales, fmt):
    g, p, n, _ = words.shape
    if fmt in ("e4m3", "e5m2"):
        vals = np.ascontiguousarray(words).view(ml_dtypes.float8_e4m3fn if fmt == "e4m3" else ml_dtypes.float8_e5m2).astype(np.float64)
    else:
        nib = np.empty((g, p, n, 4), np.uint8)
        nib[..., 0::2] = words & 0xF
        nib[..., 1::2] = words >> 4
        vals = E2M1[nib]
    vals = vals * np.repeat(np.exp2(scales.astype(np.float64) - 127.0), 8, axis=1)[..., None]
    return vals.transpose(0, 1, 3, 2).reshape(g * 512, n)

def planes(Y):
    n, m = Y.shape
    b = f64(bf(Y)).reshape(n // 32, 32, m)
    amax = np.abs(b).max(1)
    byte = np.clip(np.where(amax > 0, np.frexp(amax)[1] - 1 + 127 - 7, 1), 1, 254)
    codes = (b * np.exp2(127.0 - byte)[:, None, :]).reshape(n, m).astype(np.float32).astype(ml_dtypes.float8_e4m3fn).view(np.uint8)
    words = codes.reshape(n // 512, 128, 4, m).transpose(0, 1, 3, 2)
    return np.ascontiguousarray(words), np.ascontiguousarray(byte.astype(np.uint8).reshape(n // 512, 16, m))


M, K, N = 2048, 1536, 1024


def silu(a):
    return 0.5 * a * (1.0 + np.tanh(0.5 * a))


def setup_inputs():
    s = mx_kscale(K)
    spread = np.exp(0.7 * np.random.randn(N))
    a = np.random.randn(K, M) * np.exp(np.random.randn(K, M))
    C = silu(a)
    control_words, control_scales = pack_weight(C * s[:, None], "e5m2")
    zero_weight = 0.5 * np.random.randn(K, N) * spread / np.sqrt(K)
    return {
        "control_words": control_words,
        "control_scales": control_scales,
        "zero_weight": bf(zero_weight / s[:, None]),
        "zero_bias": bf(0.4 * np.random.randn(N) * spread),
        "strength": bf(0.4 + np.random.rand(M)),
        "skip": bf(np.random.randn(M, N) * spread),
    }


def reference(control_words, control_scales, zero_weight, zero_bias, strength, skip):
    C = unpack_weight(control_words, control_scales, "e5m2")
    W = mxq(f64(zero_weight), 0, "e4m3")
    z = C.T @ W
    r = z + f64(zero_bias)
    y = f64(skip) + f64(strength)[:, None] * r
    Y = y.T
    words, scales = planes(Y)
    return y, words, scales

@@ -1,0 +1,281 @@
+from contextlib import ExitStack
+
+import concourse.mybir as mybir
+from concourse.masks import make_identity
+
+M, K, N = 2048, 1536, 1024
+FLOPS = 2 * M * K * N
+
+F32 = mybir.dt.float32
+BF16 = mybir.dt.bfloat16
+I32 = mybir.dt.int32
+U32 = mybir.dt.uint32
+U8 = mybir.dt.uint8
+E4M3X4 = mybir.dt.float8_e4m3fn_x4
+E5M2X4 = mybir.dt.float8_e5m2_x4
+MULT = mybir.AluOpType.mult
+ADD = mybir.AluOpType.add
+
+P = 128
+PACK = 4
+GROUP = P * PACK
+PASSES = K // GROUP
+HALVES = N // GROUP
+M_TILES = M // P
+UNITS = HALVES * M_TILES
+PAIRS = UNITS // 2
+PAIRS_PER_HALF = PAIRS // HALVES
+BLOCK = 512
+BLOCKS = M // BLOCK
+TILES_PER_BLOCK = BLOCK // P
+BIAS_ROWS = N // P
+VEC_ROWS = M_TILES + BIAS_ROWS
+
+
+def tile_controlnet_zero_conv_skip_k2_kernel(
+    tc, control_words, control_scales, zero_weight, zero_bias, strength, skip, out_0, out_1, out_2
+):
+    nc = tc.nc
+    with ExitStack() as ctx:
+        keep = ctx.enter_context(tc.tile_pool(name="keep", bufs=1))
+        work = ctx.enter_context(tc.tile_pool(name="work", bufs=2))
+        psum = ctx.enter_context(tc.psum_pool(name="psum", bufs=1))
+        ctx.enter_context(tc.manual_schedule())
+
+        ident = keep.tile([P, P], F32, name="ident")
+        make_identity(nc, ident[:])
+
+        first_scales = keep.tile([P, PASSES, BLOCK], U8, name="first_scales", align_bytes=64)
+        rest_scales = keep.tile([P, PASSES, M - BLOCK], U8, name="rest_scales", align_bytes=64)
+        vec_rows = keep.tile([P, P], BF16, name="vec_rows")
+        vec_wide = keep.tile([P, P], F32, name="vec_wide")
+        vec_cols = keep.tile([P, VEC_ROWS], F32, name="vec_cols")
+        nc.vector.memset(first_scales[:].bitcast(I32), 0)
+        nc.vector.memset(vec_wide[:], 0.0)
+        nc.vector.memset(rest_scales[:].bitcast(I32), 0)
+
+        w_raw, w_codes, w_scales, w_grouped = {}, {}, {}, {}
+        c_words, skip_sb = {}, {}
+
+        def load_w(h, g):
+            w_raw[h, g] = keep.tile([P, PACK, GROUP], BF16, name="w_raw_%d_%d" % (h, g))
+            rows = zero_weight[g * GROUP : (g + 1) * GROUP, h * GROUP : (h + 1) * GROUP]
+            nc.sync.dma_start(out=w_raw[h, g][:], in_=rows.rearrange("(p t) n -> p t n", t=PACK))
+
+        def load_skip(h, b):
+            skip_sb[h, b] = keep.tile([P, TILES_PER_BLOCK, GROUP], BF16, name="skip_%d_%d" % (h, b))
+            rows = skip[b * BLOCK : (b + 1) * BLOCK, h * GROUP : (h + 1) * GROUP]
+            nc.sync.dma_start(out=skip_sb[h, b][:], in_=rows.rearrange("(a p) n -> p a n", p=P))
+
+        def load_c(b):
+            c_words[b] = keep.tile([P, PASSES, BLOCK], U32, name="c_words_%d" % b, align_bytes=64)
+            src = control_words.rearrange("g p m t -> p g (m t)")[:, :, PACK * b * BLOCK : PACK * (b + 1) * BLOCK]
+            nc.sync.dma_start(out=c_words[b][:].bitcast(I32), in_=src.bitcast(I32))
+
+        def load_c_scales(plane, m0, m1):
+            for q in range(4):
+                src = control_scales[:, 4 * q : 4 * q + 4, m0:m1].rearrange("g r m -> r g m")
+                nc.sync.dma_start(out=plane[32 * q : 32 * q + 4, :, :].bitcast(I32), in_=src.bitcast(I32))
+
+        nc.sync.dma_start(out=vec_rows[0:M_TILES, :], in_=strength.rearrange("(i p) -> i p", p=P))
+        nc.sync.dma_start(out=vec_rows[M_TILES:VEC_ROWS, :], in_=zero_bias.rearrange("(j p) -> j p", p=P))
+        load_w(0, 0)
+        load_w(0, 1)
+        load_skip(0, 0)
+        load_w(0, 2)
+        load_c_scales(first_scales, 0, BLOCK)
+        load_c(0)
+        load_skip(0, 1)
+        load_c_scales(rest_scales, BLOCK, M)
+        load_c(1)
+        load_w(1, 0)
+        load_skip(0, 2)
+        load_w(1, 1)
+        load_c(2)
+        load_w(1, 2)
+        load_skip(0, 3)
+        load_c(3)
+        for b in range(BLOCKS):
+            load_skip(1, b)
+
+        nc.vector.tensor_copy(out=vec_wide[0:VEC_ROWS, :], in_=vec_rows[0:VEC_ROWS, :])
+        vec_turned = psum.tile([P, 4, P], F32, name="vec_turned", tag="turned", bufs=2)
+        nc.tensor.transpose(vec_turned[:, 0, :], vec_wide[:], ident[:])
+        nc.scalar.copy(out=vec_cols[:], in_=vec_turned[:, 0, 0:VEC_ROWS])
+        bias_bank = []
+        for h in range(HALVES):
+            bank = psum.tile([P, GROUP], F32, name="bias_%d" % h)
+            for j in range(PACK):
+                col = M_TILES + PACK * h + j
+                nc.tensor.transpose(
+                    bank[:, j * P : (j + 1) * P], vec_cols[:, col : col + 1].to_broadcast([P, P]), ident[:]
+                )
+            bias_bank.append(bank)
+
+        def interleave_w(copy, h, g, c0, c1):
+            if c0 == 0:
+                w_grouped[h, g] = work.tile(
+                    [P, GROUP, PACK], BF16, name="w_grouped_%d_%d" % (h, g), tag="w_grouped", bufs=3, align_bytes=64
+                )
+            copy(
+                out=w_grouped[h, g][:, c0:c1, :].rearrange("p (c i) t -> p c t i", i=4),
+                in_=w_raw[h, g][:, :, c0:c1].rearrange("p t (c i) -> p c t i", i=4),
+            )
+
+        def quantize_w(h, g):
+            w_codes[h, g] = keep.tile([P, GROUP], U32, name="w_codes_%d_%d" % (h, g), align_bytes=64)
+            w_scales[h, g] = keep.tile([P, GROUP], U8, name="w_scales_%d_%d" % (h, g), align_bytes=64)
+            nc.vector.quantize_mx(
+                out=w_codes[h, g][:].bitcast(E4M3X4),
+                scales=w_scales[h, g][:],
+                in_=w_grouped[h, g][:].rearrange("p n t -> p (n t)"),
+            )
+
+        z, base, y, y_sorted, y_grouped = {}, {}, {}, {}, {}
+        y_codes = [keep.tile([P, M], U32, name="y_codes_%d" % h, align_bytes=64) for h in range(HALVES)]
+        y_scales = [keep.tile([P, M], U8, name="y_scales_%d" % h, align_bytes=64) for h in range(HALVES)]
+
+        def multiply(unit):
+            h, i = divmod(unit, M_TILES)
+            b, a = divmod(i, TILES_PER_BLOCK)
+            plane, m0 = (first_scales, i * P) if b == 0 else (rest_scales, i * P - BLOCK)
+            z[unit] = psum.tile([P, GROUP], F32, name="z_%d" % unit, tag="z", bufs=4)
+            for g in range(PASSES):
+                nc.tensor.matmul_mx(
+                    out=z[unit][:],
+                    lhsT=c_words[b][:, g, a * P : (a + 1) * P].bitcast(E5M2X4),
+                    lhsT_scale=plane[:, g, m0 : m0 + P],
+                    rhs=w_codes[h, g][:].bitcast(E4M3X4),
+                    rhs_scale=w_scales[h, g][:],
+                    start=(g == 0),
+                    stop=(g == PASSES - 1),
+                )
+
+        def make_base(unit):
+            h, i = divmod(unit, M_TILES)
+            b, a = divmod(i, TILES_PER_BLOCK)
+            base[unit] = work.tile([P, GROUP], F32, name="base_%d" % unit, tag="base", bufs=6)
+            nc.vector.scalar_tensor_tensor(
+                out=base[unit][:], in0=bias_bank[h][:], scalar=vec_cols[:, i : i + 1],
+                in1=skip_sb[h, b][:, a, :], op0=MULT, op1=ADD,
+            )
+
+        def finish(unit):
+            i = unit % M_TILES
+            pair, a = divmod(unit, 2)
+            if a == 0:
+                y[pair] = work.tile([P, 2, GROUP], F32, name="y_%d" % pair, tag="y", bufs=12)
+            nc.vector.scalar_tensor_tensor(
+                out=y[pair][:, a, :], in0=z[unit][:], scalar=vec_cols[:, i : i + 1],
+                in1=base[unit][:], op0=MULT, op1=ADD,
+            )
+
+        def round_sorted(unit):
+            pair, a = divmod(unit, 2)
+            y_sorted[unit] = work.tile([P, 2, P, 2], BF16, name="y_sorted_%d" % unit, tag="y_sorted", bufs=8)
+            nc.scalar.copy(out=y_sorted[unit][:], in_=y[pair][:, a, :].rearrange("m (p u e) -> m u p e", u=2, e=2))
+
+        def turn(pair):
+            turned = psum.tile([P, 4, P], F32, name="turned_%d" % pair, tag="turned", bufs=2)
+            for a in range(2):
+                words = y_sorted[2 * pair + a][:].rearrange("m u p e -> m (u p e)").bitcast(F32)
+                for u in range(2):
+                    nc.tensor.transpose(turned[:, 2 * a + u, :], words[:, u * P : (u + 1) * P], ident[:])
+            y_grouped[pair] = work.tile(
+                [P, 2 * P * PACK], BF16, name="y_grouped_%d" % pair, tag="y_grouped", bufs=4, align_bytes=64
+            )
+            return turned
+
+        def copy_turned(pair, turned):
+            nc.scalar.copy(
+                out=y_grouped[pair][:].bitcast(F32).rearrange("p (a m u) -> p a m u", a=2, u=2),
+                in_=turned[:].rearrange("p (a u) m -> p a m u", u=2),
+            )
+
+        def quantize_y(pair):
+            h, j = divmod(pair, PAIRS_PER_HALF)
+            cols = slice(2 * P * j, 2 * P * (j + 1))
+            nc.vector.quantize_mx(
+                out=y_codes[h][:, cols].bitcast(E4M3X4), scales=y_scales[h][:, cols], in_=y_grouped[pair][:]
+            )
+
+        def store_y(pair):
+            h, j = divmod(pair, PAIRS_PER_HALF)
+            rows = out_0[2 * P * j : 2 * P * (j + 1), h * GROUP : (h + 1) * GROUP]
+            nc.sync.dma_start(out=rows.rearrange("(a p) n -> p a n", p=P), in_=y[pair][:])
+
+        def store_words(h, m0, m1):
+            dst = out_1[h].rearrange("p m t -> p (m t)")[:, PACK * m0 : PACK * m1]
+            nc.sync.dma_start(out=dst.bitcast(I32), in_=y_codes[h][:, m0:m1].bitcast(I32))
+
+        def store_scales(h, m0, m1):
+            for q in range(4):
+                nc.sync.dma_start(
+                    out=out_2[h, 4 * q : 4 * q + 4, m0:m1].bitcast(I32),
+                    in_=y_scales[h][32 * q : 32 * q + 4, m0:m1].bitcast(I32),
+                )
+
+        def store_planes(pair):
+            h, j = divmod(pair, PAIRS_PER_HALF)
+            done = 2 * P * (j + 1)
+            if pair >= PAIRS - 2:
+                store_words(h, done - 2 * P, done)
+            elif j % 2 == 1:
+                store_words(h, done - BLOCK, done)
+            if pair == PAIRS_PER_HALF - 1:
+                store_scales(h, 0, M)
+            elif pair == PAIRS - 3:
+                store_scales(h, 0, M - BLOCK)
+            elif pair == PAIRS - 1:
+                store_scales(h, M - BLOCK, M)
+
+        interleave_w(nc.vector.tensor_copy, 0, 0, 0, GROUP)
+        interleave_w(nc.scalar.copy, 0, 1, 0, GROUP)
+        interleave_w(nc.scalar.copy, 0, 2, 0, GROUP)
+        quantize_w(0, 0)
+        make_base(0)
+        make_base(1)
+        quantize_w(0, 1)
+        make_base(2)
+        make_base(3)
+        quantize_w(0, 2)
+        multiply(0)
+        multiply(1)
+
+        def turn_slot(pair):
+            return pair + (2 if pair < PAIRS_PER_HALF - 1 else 1)
+
+        w_piece_slots = [2, 2, 3, 4, 4, 5]
+        w_quantize_slots = [3, 5, 6]
+        bases_made = 4
+        for k in range(PAIRS + 3):
+            if k + 1 < PAIRS:
+                multiply(2 * k + 2)
+                multiply(2 * k + 3)
+            if 0 < k <= PAIRS:
+                round_sorted(2 * k - 1)
+            due = [pair for pair in range(PAIRS) if turn_slot(pair) == k]
+            ready = [pair for pair in range(PAIRS) if turn_slot(pair) == k - 1]
+            for piece in range(2 * PASSES):
+                if w_piece_slots[piece] == k:
+                    g, c = divmod(piece, 2)
+                    interleave_w(nc.scalar.copy, 1, g, c * GROUP // 2, (c + 1) * GROUP // 2)
+            if k < PAIRS:
+                finish(2 * k)
+                round_sorted(2 * k)
+            for pair in due:
+                copy_turned(pair, turn(pair))
+            if k < PAIRS and bases_made < UNITS:
+                make_base(bases_made)
+                bases_made = bases_made + 1
+            for pair in ready:
+                quantize_y(pair)
+                store_planes(pair)
+            if k < PAIRS:
+                finish(2 * k + 1)
+                store_y(k)
+            if k in w_quantize_slots:
+                quantize_w(1, w_quantize_slots.index(k))
+            if k < PAIRS and bases_made < UNITS and k not in w_quantize_slots[:2]:
+                make_base(bases_made)
+                bases_made = bases_made + 1

@@ -21,15 +21,16 @@ PACK = 4
 GROUP = P * PACK
 PASSES = K // GROUP
 HALVES = N // GROUP
-M_TILES = M // P
-UNITS = HALVES * M_TILES
-PAIRS = UNITS // 2
-PAIRS_PER_HALF = PAIRS // HALVES
-BLOCK = 512
-BLOCKS = M // BLOCK
-TILES_PER_BLOCK = BLOCK // P
+TILES = M // P
+UNITS = HALVES * TILES
 BIAS_ROWS = N // P
-VEC_ROWS = M_TILES + BIAS_ROWS
+VEC_ROWS = TILES + BIAS_ROWS
+ALIGN = 256
+WORD_LOADS = [(0, 2), (2, 4), (4, 8), (8, 16)]
+SCALE_LOADS = [(0, 4), (4, 16)]
+SKIP_LOADS = [(0, 2), (2, 4), (4, 8), (8, 12), (12, 16)]
+WORD_STORES = [(0, 8), (8, 12), (12, 14), (14, 16)]
+SCALE_STORES = [(0, 12), (12, 16)]
 
 
 def tile_controlnet_zero_conv_skip_k2_kernel(
@@ -45,58 +46,65 @@ def tile_controlnet_zero_conv_skip_k2_kernel(
         ident = keep.tile([P, P], F32, name="ident")
         make_identity(nc, ident[:])
 
-        first_scales = keep.tile([P, PASSES, BLOCK], U8, name="first_scales", align_bytes=64)
-        rest_scales = keep.tile([P, PASSES, M - BLOCK], U8, name="rest_scales", align_bytes=64)
+        c_scales = [
+            keep.tile([P, PASSES, (i1 - i0) * P], U8, name="c_scales_%d" % i0, align_bytes=ALIGN)
+            for i0, i1 in SCALE_LOADS
+        ]
         vec_rows = keep.tile([P, P], BF16, name="vec_rows")
         vec_wide = keep.tile([P, P], F32, name="vec_wide")
         vec_cols = keep.tile([P, VEC_ROWS], F32, name="vec_cols")
-        nc.vector.memset(first_scales[:].bitcast(I32), 0)
         nc.vector.memset(vec_wide[:], 0.0)
-        nc.vector.memset(rest_scales[:].bitcast(I32), 0)
+        for plane in c_scales:
+            nc.vector.memset(plane[:].bitcast(I32), 0)
 
         w_raw, w_codes, w_scales, w_grouped = {}, {}, {}, {}
         c_words, skip_sb = {}, {}
 
-        def load_w(h, g):
-            w_raw[h, g] = keep.tile([P, PACK, GROUP], BF16, name="w_raw_%d_%d" % (h, g))
-            rows = zero_weight[g * GROUP : (g + 1) * GROUP, h * GROUP : (h + 1) * GROUP]
-            nc.sync.dma_start(out=w_raw[h, g][:], in_=rows.rearrange("(p t) n -> p t n", t=PACK))
+        def load_w(g, h0, h1):
+            raw = keep.tile([P, PACK, (h1 - h0) * GROUP], BF16, name="w_raw_%d_%d" % (g, h0), align_bytes=ALIGN)
+            rows = zero_weight[g * GROUP : (g + 1) * GROUP, h0 * GROUP : h1 * GROUP]
+            nc.sync.dma_start(out=raw[:], in_=rows.rearrange("(p t) n -> p t n", t=PACK))
+            for h in range(h0, h1):
+                w_raw[g, h] = raw[:, :, (h - h0) * GROUP : (h - h0 + 1) * GROUP]
 
-        def load_skip(h, b):
-            skip_sb[h, b] = keep.tile([P, TILES_PER_BLOCK, GROUP], BF16, name="skip_%d_%d" % (h, b))
-            rows = skip[b * BLOCK : (b + 1) * BLOCK, h * GROUP : (h + 1) * GROUP]
-            nc.sync.dma_start(out=skip_sb[h, b][:], in_=rows.rearrange("(a p) n -> p a n", p=P))
+        def load_skip(n):
+            i0, i1 = SKIP_LOADS[n]
+            rows = keep.tile([P, i1 - i0, N], BF16, name="skip_%d" % i0, align_bytes=ALIGN)
+            nc.sync.dma_start(out=rows[:], in_=skip[i0 * P : i1 * P, :].rearrange("(a p) n -> p a n", p=P))
+            for i in range(i0, i1):
+                skip_sb[i] = rows[:, i - i0, :]
 
-        def load_c(b):
-            c_words[b] = keep.tile([P, PASSES, BLOCK], U32, name="c_words_%d" % b, align_bytes=64)
-            src = control_words.rearrange("g p m t -> p g (m t)")[:, :, PACK * b * BLOCK : PACK * (b + 1) * BLOCK]
-            nc.sync.dma_start(out=c_words[b][:].bitcast(I32), in_=src.bitcast(I32))
+        def load_words(n):
+            i0, i1 = WORD_LOADS[n]
+            words = keep.tile([P, PASSES, (i1 - i0) * P], U32, name="c_words_%d" % i0, align_bytes=ALIGN)
+            src = control_words.rearrange("g p m t -> p g (m t)")[:, :, PACK * i0 * P : PACK * i1 * P]
+            nc.sync.dma_start(out=words[:].bitcast(I32), in_=src.bitcast(I32))
+            for i in range(i0, i1):
+                c_words[i] = words[:, :, (i - i0) * P : (i - i0 + 1) * P]
 
-        def load_c_scales(plane, m0, m1):
+        def load_scales(n):
+            i0, i1 = SCALE_LOADS[n]
             for q in range(4):
-                src = control_scales[:, 4 * q : 4 * q + 4, m0:m1].rearrange("g r m -> r g m")
-                nc.sync.dma_start(out=plane[32 * q : 32 * q + 4, :, :].bitcast(I32), in_=src.bitcast(I32))
+                src = control_scales[:, 4 * q : 4 * q + 4, i0 * P : i1 * P].rearrange("g r m -> r g m")
+                nc.sync.dma_start(out=c_scales[n][32 * q : 32 * q + 4, :, :].bitcast(I32), in_=src.bitcast(I32))
 
-        nc.sync.dma_start(out=vec_rows[0:M_TILES, :], in_=strength.rearrange("(i p) -> i p", p=P))
-        nc.sync.dma_start(out=vec_rows[M_TILES:VEC_ROWS, :], in_=zero_bias.rearrange("(j p) -> j p", p=P))
-        load_w(0, 0)
-        load_w(0, 1)
-        load_skip(0, 0)
-        load_w(0, 2)
-        load_c_scales(first_scales, 0, BLOCK)
-        load_c(0)
-        load_skip(0, 1)
-        load_c_scales(rest_scales, BLOCK, M)
-        load_c(1)
-        load_w(1, 0)
-        load_skip(0, 2)
-        load_w(1, 1)
-        load_c(2)
-        load_w(1, 2)
-        load_skip(0, 3)
-        load_c(3)
-        for b in range(BLOCKS):
-            load_skip(1, b)
+        nc.sync.dma_start(out=vec_rows[0:TILES, :], in_=strength.rearrange("(i p) -> i p", p=P))
+        nc.sync.dma_start(out=vec_rows[TILES:VEC_ROWS, :], in_=zero_bias.rearrange("(j p) -> j p", p=P))
+        load_w(0, 0, 1)
+        load_w(0, 1, 2)
+        load_w(1, 0, 2)
+        load_w(2, 0, 2)
+        load_skip(0)
+        load_scales(0)
+        load_words(0)
+        load_skip(1)
+        load_words(1)
+        load_scales(1)
+        load_skip(2)
+        load_words(2)
+        load_words(3)
+        load_skip(3)
+        load_skip(4)
 
         nc.vector.tensor_copy(out=vec_wide[0:VEC_ROWS, :], in_=vec_rows[0:VEC_ROWS, :])
         vec_turned = psum.tile([P, 4, P], F32, name="vec_turned", tag="turned", bufs=2)
@@ -106,176 +114,153 @@ def tile_controlnet_zero_conv_skip_k2_kernel(
         for h in range(HALVES):
             bank = psum.tile([P, GROUP], F32, name="bias_%d" % h)
             for j in range(PACK):
-                col = M_TILES + PACK * h + j
+                col = TILES + PACK * h + j
                 nc.tensor.transpose(
                     bank[:, j * P : (j + 1) * P], vec_cols[:, col : col + 1].to_broadcast([P, P]), ident[:]
                 )
             bias_bank.append(bank)
 
-        def interleave_w(copy, h, g, c0, c1):
-            if c0 == 0:
-                w_grouped[h, g] = work.tile(
-                    [P, GROUP, PACK], BF16, name="w_grouped_%d_%d" % (h, g), tag="w_grouped", bufs=3, align_bytes=64
-                )
+        def interleave_w(copy, g, h):
+            w_grouped[g, h] = work.tile(
+                [P, GROUP, PACK], BF16, name="w_grouped_%d_%d" % (g, h), tag="w_grouped", bufs=4, align_bytes=ALIGN
+            )
             copy(
-                out=w_grouped[h, g][:, c0:c1, :].rearrange("p (c i) t -> p c t i", i=4),
-                in_=w_raw[h, g][:, :, c0:c1].rearrange("p t (c i) -> p c t i", i=4),
+                out=w_grouped[g, h][:].rearrange("p (c i) t -> p c t i", i=4),
+                in_=w_raw[g, h].rearrange("p t (c i) -> p c t i", i=4),
             )
 
-        def quantize_w(h, g):
-            w_codes[h, g] = keep.tile([P, GROUP], U32, name="w_codes_%d_%d" % (h, g), align_bytes=64)
-            w_scales[h, g] = keep.tile([P, GROUP], U8, name="w_scales_%d_%d" % (h, g), align_bytes=64)
+        def quantize_w(g, h):
+            w_codes[g, h] = keep.tile([P, GROUP], U32, name="w_codes_%d_%d" % (g, h), align_bytes=ALIGN)
+            w_scales[g, h] = keep.tile([P, GROUP], U8, name="w_scales_%d_%d" % (g, h), align_bytes=ALIGN)
             nc.vector.quantize_mx(
-                out=w_codes[h, g][:].bitcast(E4M3X4),
-                scales=w_scales[h, g][:],
-                in_=w_grouped[h, g][:].rearrange("p n t -> p (n t)"),
+                out=w_codes[g, h][:].bitcast(E4M3X4),
+                scales=w_scales[g, h][:],
+                in_=w_grouped[g, h][:].rearrange("p n t -> p (n t)"),
             )
 
         z, base, y, y_sorted, y_grouped = {}, {}, {}, {}, {}
-        y_codes = [keep.tile([P, M], U32, name="y_codes_%d" % h, align_bytes=64) for h in range(HALVES)]
-        y_scales = [keep.tile([P, M], U8, name="y_scales_%d" % h, align_bytes=64) for h in range(HALVES)]
+        y_codes = keep.tile([P, HALVES, M], U32, name="y_codes", align_bytes=ALIGN)
+        y_scales = keep.tile([P, M], U8, name="y_scales", align_bytes=ALIGN)
 
         def multiply(unit):
-            h, i = divmod(unit, M_TILES)
-            b, a = divmod(i, TILES_PER_BLOCK)
-            plane, m0 = (first_scales, i * P) if b == 0 else (rest_scales, i * P - BLOCK)
+            i, h = divmod(unit, HALVES)
+            n = 0 if i < SCALE_LOADS[0][1] else 1
+            m0 = (i - SCALE_LOADS[n][0]) * P
             z[unit] = psum.tile([P, GROUP], F32, name="z_%d" % unit, tag="z", bufs=4)
             for g in range(PASSES):
                 nc.tensor.matmul_mx(
                     out=z[unit][:],
-                    lhsT=c_words[b][:, g, a * P : (a + 1) * P].bitcast(E5M2X4),
-                    lhsT_scale=plane[:, g, m0 : m0 + P],
-                    rhs=w_codes[h, g][:].bitcast(E4M3X4),
-                    rhs_scale=w_scales[h, g][:],
+                    lhsT=c_words[i][:, g, :].bitcast(E5M2X4),
+                    lhsT_scale=c_scales[n][:, g, m0 : m0 + P],
+                    rhs=w_codes[g, h][:].bitcast(E4M3X4),
+                    rhs_scale=w_scales[g, h][:],
                     start=(g == 0),
                     stop=(g == PASSES - 1),
                 )
 
         def make_base(unit):
-            h, i = divmod(unit, M_TILES)
-            b, a = divmod(i, TILES_PER_BLOCK)
-            base[unit] = work.tile([P, GROUP], F32, name="base_%d" % unit, tag="base", bufs=6)
+            i, h = divmod(unit, HALVES)
+            base[unit] = work.tile([P, GROUP], F32, name="base_%d" % unit, tag="base", bufs=4)
             nc.vector.scalar_tensor_tensor(
                 out=base[unit][:], in0=bias_bank[h][:], scalar=vec_cols[:, i : i + 1],
-                in1=skip_sb[h, b][:, a, :], op0=MULT, op1=ADD,
+                in1=skip_sb[i][:, h * GROUP : (h + 1) * GROUP], op0=MULT, op1=ADD,
             )
 
         def finish(unit):
-            i = unit % M_TILES
-            pair, a = divmod(unit, 2)
-            if a == 0:
-                y[pair] = work.tile([P, 2, GROUP], F32, name="y_%d" % pair, tag="y", bufs=12)
+            i, h = divmod(unit, HALVES)
+            if h == 0:
+                y[i] = work.tile([P, N], F32, name="y_%d" % i, tag="y", bufs=10, align_bytes=ALIGN)
             nc.vector.scalar_tensor_tensor(
-                out=y[pair][:, a, :], in0=z[unit][:], scalar=vec_cols[:, i : i + 1],
+                out=y[i][:, h * GROUP : (h + 1) * GROUP], in0=z[unit][:], scalar=vec_cols[:, i : i + 1],
                 in1=base[unit][:], op0=MULT, op1=ADD,
             )
 
-        def round_sorted(unit):
-            pair, a = divmod(unit, 2)
-            y_sorted[unit] = work.tile([P, 2, P, 2], BF16, name="y_sorted_%d" % unit, tag="y_sorted", bufs=8)
-            nc.scalar.copy(out=y_sorted[unit][:], in_=y[pair][:, a, :].rearrange("m (p u e) -> m u p e", u=2, e=2))
+        def round_sorted(copy, unit):
+            i, h = divmod(unit, HALVES)
+            y_sorted[unit] = work.tile([P, 2, P, 2], BF16, name="y_sorted_%d" % unit, tag="y_sorted", bufs=6)
+            copy(
+                out=y_sorted[unit][:],
+                in_=y[i][:, h * GROUP : (h + 1) * GROUP].rearrange("m (p u e) -> m u p e", u=2, e=2),
+            )
 
-        def turn(pair):
-            turned = psum.tile([P, 4, P], F32, name="turned_%d" % pair, tag="turned", bufs=2)
-            for a in range(2):
-                words = y_sorted[2 * pair + a][:].rearrange("m u p e -> m (u p e)").bitcast(F32)
+        def turn(i, h0, h1):
+            turned = psum.tile([P, h1 - h0, 2, P], F32, name="turned_%d_%d" % (i, h0), tag="turned", bufs=2)
+            for h in range(h0, h1):
+                words = y_sorted[HALVES * i + h][:].rearrange("m u p e -> m (u p e)").bitcast(F32)
                 for u in range(2):
-                    nc.tensor.transpose(turned[:, 2 * a + u, :], words[:, u * P : (u + 1) * P], ident[:])
-            y_grouped[pair] = work.tile(
-                [P, 2 * P * PACK], BF16, name="y_grouped_%d" % pair, tag="y_grouped", bufs=4, align_bytes=64
-            )
-            return turned
-
-        def copy_turned(pair, turned):
-            nc.scalar.copy(
-                out=y_grouped[pair][:].bitcast(F32).rearrange("p (a m u) -> p a m u", a=2, u=2),
-                in_=turned[:].rearrange("p (a u) m -> p a m u", u=2),
-            )
-
-        def quantize_y(pair):
-            h, j = divmod(pair, PAIRS_PER_HALF)
-            cols = slice(2 * P * j, 2 * P * (j + 1))
-            nc.vector.quantize_mx(
-                out=y_codes[h][:, cols].bitcast(E4M3X4), scales=y_scales[h][:, cols], in_=y_grouped[pair][:]
-            )
-
-        def store_y(pair):
-            h, j = divmod(pair, PAIRS_PER_HALF)
-            rows = out_0[2 * P * j : 2 * P * (j + 1), h * GROUP : (h + 1) * GROUP]
-            nc.sync.dma_start(out=rows.rearrange("(a p) n -> p a n", p=P), in_=y[pair][:])
-
-        def store_words(h, m0, m1):
-            dst = out_1[h].rearrange("p m t -> p (m t)")[:, PACK * m0 : PACK * m1]
-            nc.sync.dma_start(out=dst.bitcast(I32), in_=y_codes[h][:, m0:m1].bitcast(I32))
-
-        def store_scales(h, m0, m1):
-            for q in range(4):
-                nc.sync.dma_start(
-                    out=out_2[h, 4 * q : 4 * q + 4, m0:m1].bitcast(I32),
-                    in_=y_scales[h][32 * q : 32 * q + 4, m0:m1].bitcast(I32),
+                    nc.tensor.transpose(turned[:, h - h0, u, :], words[:, u * P : (u + 1) * P], ident[:])
+            pair, a = divmod(i, 2)
+            if a == 0 and h0 == 0:
+                y_grouped[pair] = work.tile(
+                    [P, HALVES, 2 * P * PACK], BF16, name="y_grouped_%d" % pair, tag="y_grouped", bufs=3,
+                    align_bytes=ALIGN,
                 )
+            words_out = y_grouped[pair][:].bitcast(F32).rearrange("p h (m u) -> p h m u", u=2)
+            nc.scalar.copy(
+                out=words_out[:, h0:h1, a * P : (a + 1) * P, :], in_=turned[:].rearrange("p h u m -> p h m u")
+            )
 
-        def store_planes(pair):
-            h, j = divmod(pair, PAIRS_PER_HALF)
-            done = 2 * P * (j + 1)
-            if pair >= PAIRS - 2:
-                store_words(h, done - 2 * P, done)
-            elif j % 2 == 1:
-                store_words(h, done - BLOCK, done)
-            if pair == PAIRS_PER_HALF - 1:
-                store_scales(h, 0, M)
-            elif pair == PAIRS - 3:
-                store_scales(h, 0, M - BLOCK)
-            elif pair == PAIRS - 1:
-                store_scales(h, M - BLOCK, M)
+        def quantize_y(pair, h):
+            cols = slice(2 * P * pair, 2 * P * (pair + 1))
+            nc.vector.quantize_mx(
+                out=y_codes[:, h, cols].bitcast(E4M3X4), scales=y_scales[4 * h : P, cols], in_=y_grouped[pair][:, h, :]
+            )
 
-        interleave_w(nc.vector.tensor_copy, 0, 0, 0, GROUP)
-        interleave_w(nc.scalar.copy, 0, 1, 0, GROUP)
-        interleave_w(nc.scalar.copy, 0, 2, 0, GROUP)
-        quantize_w(0, 0)
+        def store_y(i):
+            nc.sync.dma_start(out=out_0[i * P : (i + 1) * P, :], in_=y[i][:])
+
+        def store_planes(tiles_done):
+            for i0, i1 in WORD_STORES:
+                if i1 == tiles_done:
+                    dst = out_1.rearrange("h p m t -> p h (m t)")[:, :, PACK * i0 * P : PACK * i1 * P]
+                    nc.sync.dma_start(out=dst.bitcast(I32), in_=y_codes[:, :, i0 * P : i1 * P].bitcast(I32))
+            for i0, i1 in SCALE_STORES:
+                if i1 == tiles_done:
+                    for q in range(4):
+                        nc.sync.dma_start(
+                            out=out_2[:, 4 * q : 4 * q + 4, i0 * P : i1 * P].bitcast(I32),
+                            in_=y_scales[32 * q : 32 * q + 4 * HALVES, i0 * P : i1 * P].bitcast(I32),
+                        )
+
+        for g in range(PASSES):
+            interleave_w(nc.vector.tensor_copy, g, 0)
+            interleave_w(nc.scalar.copy, g, 1)
+            if g > 0:
+                quantize_w(g - 1, 1)
+            quantize_w(g, 0)
         make_base(0)
+        quantize_w(PASSES - 1, 1)
         make_base(1)
-        quantize_w(0, 1)
-        make_base(2)
-        make_base(3)
-        quantize_w(0, 2)
         multiply(0)
         multiply(1)
 
-        def turn_slot(pair):
-            return pair + (2 if pair < PAIRS_PER_HALF - 1 else 1)
-
-        w_piece_slots = [2, 2, 3, 4, 4, 5]
-        w_quantize_slots = [3, 5, 6]
-        bases_made = 4
-        for k in range(PAIRS + 3):
-            if k + 1 < PAIRS:
-                multiply(2 * k + 2)
-                multiply(2 * k + 3)
-            if 0 < k <= PAIRS:
-                round_sorted(2 * k - 1)
-            due = [pair for pair in range(PAIRS) if turn_slot(pair) == k]
-            ready = [pair for pair in range(PAIRS) if turn_slot(pair) == k - 1]
-            for piece in range(2 * PASSES):
-                if w_piece_slots[piece] == k:
-                    g, c = divmod(piece, 2)
-                    interleave_w(nc.scalar.copy, 1, g, c * GROUP // 2, (c + 1) * GROUP // 2)
-            if k < PAIRS:
-                finish(2 * k)
-                round_sorted(2 * k)
-            for pair in due:
-                copy_turned(pair, turn(pair))
-            if k < PAIRS and bases_made < UNITS:
-                make_base(bases_made)
-                bases_made = bases_made + 1
-            for pair in ready:
-                quantize_y(pair)
-                store_planes(pair)
-            if k < PAIRS:
-                finish(2 * k + 1)
-                store_y(k)
-            if k in w_quantize_slots:
-                quantize_w(1, w_quantize_slots.index(k))
-            if k < PAIRS and bases_made < UNITS and k not in w_quantize_slots[:2]:
-                make_base(bases_made)
-                bases_made = bases_made + 1
+        last = TILES - 1
+        for i in range(TILES):
+            if i < last:
+                multiply(2 * i + 2)
+                multiply(2 * i + 3)
+            if i > 0:
+                round_sorted(nc.scalar.copy, 2 * i - 1)
+            finish(2 * i)
+            round_sorted(nc.scalar.copy, 2 * i)
+            if i > 0:
+                turn(i - 1, 0, HALVES)
+            if i < last:
+                make_base(2 * i + 2)
+            if i >= 3:
+                pair, h = divmod(i - 3, 2)
+                quantize_y(pair, h)
+                if h == 1:
+                    store_planes(2 * pair + 2)
+            finish(2 * i + 1)
+            store_y(i)
+            if i < last:
+                make_base(2 * i + 3)
+        pair = TILES // 2 - 1
+        quantize_y(pair - 1, 1)
+        store_planes(TILES - 2)
+        round_sorted(nc.vector.tensor_copy, UNITS - 1)
+        for h in range(HALVES):
+            turn(last, h, h + 1)
+            quantize_y(pair, h)
+        store_planes(TILES)

@@ -15,6 +15,7 @@ E4M3X4 = mybir.dt.float8_e4m3fn_x4
 E5M2X4 = mybir.dt.float8_e5m2_x4
 MULT = mybir.AluOpType.mult
 ADD = mybir.AluOpType.add
+COPY = mybir.ActivationFunctionType.Copy
 
 P = 128
 PACK = 4
@@ -28,7 +29,7 @@ VEC_ROWS = TILES + BIAS_ROWS
 ALIGN = 256
 WORD_LOADS = [(0, 2), (2, 4), (4, 8), (8, 16)]
 SCALE_LOADS = [(0, 4), (4, 16)]
-SKIP_LOADS = [(0, 2), (2, 4), (4, 8), (8, 12), (12, 16)]
+SKIP_LOADS = [(0, 2), (2, 4), (4, 6), (6, 8), (8, 12), (12, 16)]
 WORD_STORES = [(0, 8), (8, 12), (12, 14), (14, 16)]
 SCALE_STORES = [(0, 12), (12, 16)]
 
@@ -88,37 +89,39 @@ def tile_controlnet_zero_conv_skip_k2_kernel(
                 src = control_scales[:, 4 * q : 4 * q + 4, i0 * P : i1 * P].rearrange("g r m -> r g m")
                 nc.sync.dma_start(out=c_scales[n][32 * q : 32 * q + 4, :, :].bitcast(I32), in_=src.bitcast(I32))
 
+        load_w(0, 0, 2)
         nc.sync.dma_start(out=vec_rows[0:TILES, :], in_=strength.rearrange("(i p) -> i p", p=P))
         nc.sync.dma_start(out=vec_rows[TILES:VEC_ROWS, :], in_=zero_bias.rearrange("(j p) -> j p", p=P))
-        load_w(0, 0, 1)
-        load_w(0, 1, 2)
         load_w(1, 0, 2)
-        load_w(2, 0, 2)
-        load_skip(0)
         load_scales(0)
         load_words(0)
-        load_skip(1)
+        load_w(2, 0, 2)
+        load_skip(0)
         load_words(1)
+        load_skip(1)
         load_scales(1)
         load_skip(2)
         load_words(2)
-        load_words(3)
         load_skip(3)
+        load_words(3)
         load_skip(4)
+        load_skip(5)
 
-        nc.vector.tensor_copy(out=vec_wide[0:VEC_ROWS, :], in_=vec_rows[0:VEC_ROWS, :])
-        vec_turned = psum.tile([P, 4, P], F32, name="vec_turned", tag="turned", bufs=2)
-        nc.tensor.transpose(vec_turned[:, 0, :], vec_wide[:], ident[:])
-        nc.scalar.copy(out=vec_cols[:], in_=vec_turned[:, 0, 0:VEC_ROWS])
-        bias_bank = []
-        for h in range(HALVES):
-            bank = psum.tile([P, GROUP], F32, name="bias_%d" % h)
-            for j in range(PACK):
-                col = TILES + PACK * h + j
-                nc.tensor.transpose(
-                    bank[:, j * P : (j + 1) * P], vec_cols[:, col : col + 1].to_broadcast([P, P]), ident[:]
-                )
-            bias_bank.append(bank)
+        bias_bank = [psum.tile([P, GROUP], F32, name="bias_%d" % h) for h in range(HALVES)]
+
+        def spread_vectors():
+            nc.vector.tensor_copy(out=vec_wide[0:VEC_ROWS, :], in_=vec_rows[0:VEC_ROWS, :])
+            vec_turned = psum.tile([P, 4, P], F32, name="vec_turned", tag="turned", bufs=2)
+            nc.tensor.transpose(vec_turned[:, 0, :], vec_wide[:], ident[:])
+            nc.scalar.copy(out=vec_cols[:], in_=vec_turned[:, 0, 0:VEC_ROWS])
+            for h in range(HALVES):
+                for j in range(PACK):
+                    col = TILES + PACK * h + j
+                    nc.tensor.transpose(
+                        bias_bank[h][:, j * P : (j + 1) * P],
+                        vec_cols[:, col : col + 1].to_broadcast([P, P]),
+                        ident[:],
+                    )
 
         def interleave_w(copy, g, h):
             w_grouped[g, h] = work.tile(
@@ -138,33 +141,46 @@ def tile_controlnet_zero_conv_skip_k2_kernel(
                 in_=w_grouped[g, h][:].rearrange("p n t -> p (n t)"),
             )
 
-        z, base, y, y_sorted, y_grouped = {}, {}, {}, {}, {}
+        z, base, scaled, y, y_sorted, y_grouped = {}, {}, {}, {}, {}, {}
         y_codes = keep.tile([P, HALVES, M], U32, name="y_codes", align_bytes=ALIGN)
         y_scales = keep.tile([P, M], U8, name="y_scales", align_bytes=ALIGN)
 
-        def multiply(unit):
+        def multiply_pass(unit, g):
             i, h = divmod(unit, HALVES)
             n = 0 if i < SCALE_LOADS[0][1] else 1
             m0 = (i - SCALE_LOADS[n][0]) * P
-            z[unit] = psum.tile([P, GROUP], F32, name="z_%d" % unit, tag="z", bufs=4)
+            if g == 0:
+                z[unit] = psum.tile([P, GROUP], F32, name="z_%d" % unit, tag="z", bufs=4)
+            nc.tensor.matmul_mx(
+                out=z[unit][:],
+                lhsT=c_words[i][:, g, :].bitcast(E5M2X4),
+                lhsT_scale=c_scales[n][:, g, m0 : m0 + P],
+                rhs=w_codes[g, h][:].bitcast(E4M3X4),
+                rhs_scale=w_scales[g, h][:],
+                start=(g == 0),
+                stop=(g == PASSES - 1),
+            )
+
+        def multiply(unit):
             for g in range(PASSES):
-                nc.tensor.matmul_mx(
-                    out=z[unit][:],
-                    lhsT=c_words[i][:, g, :].bitcast(E5M2X4),
-                    lhsT_scale=c_scales[n][:, g, m0 : m0 + P],
-                    rhs=w_codes[g, h][:].bitcast(E4M3X4),
-                    rhs_scale=w_scales[g, h][:],
-                    start=(g == 0),
-                    stop=(g == PASSES - 1),
-                )
+                multiply_pass(unit, g)
 
         def make_base(unit):
             i, h = divmod(unit, HALVES)
-            base[unit] = work.tile([P, GROUP], F32, name="base_%d" % unit, tag="base", bufs=4)
+            base[unit] = work.tile([P, GROUP], F32, name="base_%d" % unit, tag="base", bufs=3)
             nc.vector.scalar_tensor_tensor(
                 out=base[unit][:], in0=bias_bank[h][:], scalar=vec_cols[:, i : i + 1],
                 in1=skip_sb[i][:, h * GROUP : (h + 1) * GROUP], op0=MULT, op1=ADD,
             )
+
+        def scale_bias(i):
+            scaled[i] = work.tile([P, GROUP], F32, name="scaled_%d" % i, tag="scaled", bufs=2)
+            nc.scalar.activation(out=scaled[i][:], in_=bias_bank[1][:], func=COPY, scale=vec_cols[:, i : i + 1])
+
+        def add_skip(i):
+            unit = HALVES * i + 1
+            base[unit] = work.tile([P, GROUP], F32, name="base_%d" % unit, tag="summed", bufs=2)
+            nc.gpsimd.tensor_tensor(out=base[unit][:], in0=scaled[i][:], in1=skip_sb[i][:, GROUP:N], op=ADD)
 
         def finish(unit):
             i, h = divmod(unit, HALVES)
@@ -222,25 +238,42 @@ def tile_controlnet_zero_conv_skip_k2_kernel(
                             in_=y_scales[32 * q : 32 * q + 4 * HALVES, i0 * P : i1 * P].bitcast(I32),
                         )
 
-        for g in range(PASSES):
-            interleave_w(nc.vector.tensor_copy, g, 0)
-            interleave_w(nc.scalar.copy, g, 1)
-            if g > 0:
-                quantize_w(g - 1, 1)
-            quantize_w(g, 0)
+        first_units = range(2 * HALVES)
+        interleave_w(nc.vector.tensor_copy, 0, 0)
+        interleave_w(nc.scalar.copy, 0, 1)
+        spread_vectors()
+        quantize_w(0, 0)
+        interleave_w(nc.vector.tensor_copy, 1, 0)
+        interleave_w(nc.scalar.copy, 1, 1)
+        quantize_w(0, 1)
+        for unit in first_units:
+            multiply_pass(unit, 0)
+        for h in range(HALVES):
+            quantize_w(1, h)
+            for unit in first_units[h::HALVES]:
+                multiply_pass(unit, 1)
+        interleave_w(nc.vector.tensor_copy, 2, 0)
+        interleave_w(nc.scalar.copy, 2, 1)
         make_base(0)
-        quantize_w(PASSES - 1, 1)
+        for h in range(HALVES):
+            quantize_w(2, h)
+            for unit in first_units[h::HALVES]:
+                multiply_pass(unit, 2)
         make_base(1)
-        multiply(0)
-        multiply(1)
+        scale_bias(1)
+        add_skip(1)
 
         last = TILES - 1
         for i in range(TILES):
-            if i < last:
+            if 0 < i < last:
                 multiply(2 * i + 2)
                 multiply(2 * i + 3)
+            if 0 < i < last:
+                add_skip(i + 1)
             if i > 0:
                 round_sorted(nc.scalar.copy, 2 * i - 1)
+            if i + 2 < TILES:
+                scale_bias(i + 2)
             finish(2 * i)
             round_sorted(nc.scalar.copy, 2 * i)
             if i > 0:
@@ -254,8 +287,6 @@ def tile_controlnet_zero_conv_skip_k2_kernel(
                     store_planes(2 * pair + 2)
             finish(2 * i + 1)
             store_y(i)
-            if i < last:
-                make_base(2 * i + 3)
         pair = TILES // 2 - 1
         quantize_y(pair - 1, 1)
         store_planes(TILES - 2)

@@ -23,15 +23,21 @@ GROUP = P * PACK
 PASSES = K // GROUP
 HALVES = N // GROUP
 TILES = M // P
-UNITS = HALVES * TILES
-BIAS_ROWS = N // P
-VEC_ROWS = TILES + BIAS_ROWS
+PAIRS = TILES // 2
+QUADRANT = 32
+SCALE_ROWS = 16
+VEC_ROWS = TILES + N // P
 ALIGN = 256
-WORD_LOADS = [(0, 2), (2, 4), (4, 8), (8, 16)]
+
+WORD_LOADS = [(0, 1), (1, 4), (4, 8), (8, 16)]
 SCALE_LOADS = [(0, 4), (4, 16)]
-SKIP_LOADS = [(0, 2), (2, 4), (4, 6), (6, 8), (8, 12), (12, 16)]
-WORD_STORES = [(0, 8), (8, 12), (12, 14), (14, 16)]
-SCALE_STORES = [(0, 12), (12, 16)]
+SKIP_LOADS = [(0, 1), (1, 2), (2, 4), (4, 6), (6, 8), (8, 12), (12, 16)]
+WORD_STORES = [(0, 6), (6, 10), (10, 12), (12, 14), (14, 16)]
+SCALE_STORES = [(0, 8), (8, 16)]
+
+SCALE_AHEAD = 4
+QUANTIZE_BEHIND = 2
+VECTOR_COPY_EVERY = 4
 
 
 def tile_controlnet_zero_conv_skip_k2_kernel(
@@ -40,40 +46,39 @@ def tile_controlnet_zero_conv_skip_k2_kernel(
     nc = tc.nc
     with ExitStack() as ctx:
         keep = ctx.enter_context(tc.tile_pool(name="keep", bufs=1))
-        work = ctx.enter_context(tc.tile_pool(name="work", bufs=2))
+        work = ctx.enter_context(tc.tile_pool(name="work", bufs=1))
         psum = ctx.enter_context(tc.psum_pool(name="psum", bufs=1))
         ctx.enter_context(tc.manual_schedule())
 
         ident = keep.tile([P, P], F32, name="ident")
         make_identity(nc, ident[:])
 
-        c_scales = [
-            keep.tile([P, PASSES, (i1 - i0) * P], U8, name="c_scales_%d" % i0, align_bytes=ALIGN)
+        c_planes = [
+            keep.tile([P, PASSES, (i1 - i0) * P], U8, name="c_planes_%d" % i0, align_bytes=ALIGN)
             for i0, i1 in SCALE_LOADS
         ]
         vec_rows = keep.tile([P, P], BF16, name="vec_rows")
         vec_wide = keep.tile([P, P], F32, name="vec_wide")
         vec_cols = keep.tile([P, VEC_ROWS], F32, name="vec_cols")
         nc.vector.memset(vec_wide[:], 0.0)
-        for plane in c_scales:
+        for plane in c_planes:
             nc.vector.memset(plane[:].bitcast(I32), 0)
 
-        w_raw, w_codes, w_scales, w_grouped = {}, {}, {}, {}
-        c_words, skip_sb = {}, {}
+        w_raw, c_words, c_scales, skip_rows, skip_pair = {}, {}, {}, {}, {}
 
-        def load_w(g, h0, h1):
-            raw = keep.tile([P, PACK, (h1 - h0) * GROUP], BF16, name="w_raw_%d_%d" % (g, h0), align_bytes=ALIGN)
-            rows = zero_weight[g * GROUP : (g + 1) * GROUP, h0 * GROUP : h1 * GROUP]
-            nc.sync.dma_start(out=raw[:], in_=rows.rearrange("(p t) n -> p t n", t=PACK))
-            for h in range(h0, h1):
-                w_raw[g, h] = raw[:, :, (h - h0) * GROUP : (h - h0 + 1) * GROUP]
+        def load_w(g):
+            w_raw[g] = keep.tile([P, PACK, N], BF16, name="w_raw_%d" % g, align_bytes=ALIGN)
+            rows = zero_weight[g * GROUP : (g + 1) * GROUP, :]
+            nc.sync.dma_start(out=w_raw[g][:], in_=rows.rearrange("(p t) n -> p t n", t=PACK))
 
         def load_skip(n):
             i0, i1 = SKIP_LOADS[n]
             rows = keep.tile([P, i1 - i0, N], BF16, name="skip_%d" % i0, align_bytes=ALIGN)
             nc.sync.dma_start(out=rows[:], in_=skip[i0 * P : i1 * P, :].rearrange("(a p) n -> p a n", p=P))
             for i in range(i0, i1):
-                skip_sb[i] = rows[:, i - i0, :]
+                skip_rows[i] = rows[:, i - i0, :]
+                if i % 2 == 0 and i + 1 < i1:
+                    skip_pair[i // 2] = rows[:, i - i0 : i - i0 + 2, :]
 
         def load_words(n):
             i0, i1 = WORD_LOADS[n]
@@ -85,43 +90,51 @@ def tile_controlnet_zero_conv_skip_k2_kernel(
 
         def load_scales(n):
             i0, i1 = SCALE_LOADS[n]
-            for q in range(4):
-                src = control_scales[:, 4 * q : 4 * q + 4, i0 * P : i1 * P].rearrange("g r m -> r g m")
-                nc.sync.dma_start(out=c_scales[n][32 * q : 32 * q + 4, :, :].bitcast(I32), in_=src.bitcast(I32))
+            for r in range(4):
+                src = control_scales[:, r:SCALE_ROWS:4, i0 * P : i1 * P].rearrange("g q m -> q g m")
+                nc.sync.dma_start(out=c_planes[n][r:P:QUADRANT, :, :].bitcast(I32), in_=src.bitcast(I32))
+            for i in range(i0, i1):
+                c_scales[i] = c_planes[n][:, :, (i - i0) * P : (i - i0 + 1) * P]
 
-        load_w(0, 0, 2)
+        load_w(0)
         nc.sync.dma_start(out=vec_rows[0:TILES, :], in_=strength.rearrange("(i p) -> i p", p=P))
         nc.sync.dma_start(out=vec_rows[TILES:VEC_ROWS, :], in_=zero_bias.rearrange("(j p) -> j p", p=P))
-        load_w(1, 0, 2)
+        load_w(1)
+        load_w(2)
         load_scales(0)
         load_words(0)
-        load_w(2, 0, 2)
         load_skip(0)
         load_words(1)
         load_skip(1)
-        load_scales(1)
         load_skip(2)
-        load_words(2)
+        load_scales(1)
         load_skip(3)
-        load_words(3)
+        load_words(2)
         load_skip(4)
+        load_words(3)
         load_skip(5)
+        load_skip(6)
 
-        bias_bank = [psum.tile([P, GROUP], F32, name="bias_%d" % h) for h in range(HALVES)]
+        bias_bank = {}
+        bias_high = keep.tile([P, GROUP], F32, name="bias_high")
 
         def spread_vectors():
             nc.vector.tensor_copy(out=vec_wide[0:VEC_ROWS, :], in_=vec_rows[0:VEC_ROWS, :])
-            vec_turned = psum.tile([P, 4, P], F32, name="vec_turned", tag="turned", bufs=2)
-            nc.tensor.transpose(vec_turned[:, 0, :], vec_wide[:], ident[:])
-            nc.scalar.copy(out=vec_cols[:], in_=vec_turned[:, 0, 0:VEC_ROWS])
+            vec_turned = psum.tile([P, P], F32, name="vec_turned", tag="turned", bufs=3)
+            nc.tensor.transpose(vec_turned[:], vec_wide[:], ident[:])
+            nc.scalar.copy(out=vec_cols[:], in_=vec_turned[:, 0:VEC_ROWS])
+            bias_bank[0] = psum.tile([P, GROUP], F32, name="bias_0")
+            bias_bank[1] = psum.tile([P, GROUP], F32, name="bias_1", tag="turned", bufs=3)
             for h in range(HALVES):
-                for j in range(PACK):
-                    col = TILES + PACK * h + j
+                for j in range(GROUP // P):
+                    col = TILES + h * GROUP // P + j
                     nc.tensor.transpose(
                         bias_bank[h][:, j * P : (j + 1) * P],
                         vec_cols[:, col : col + 1].to_broadcast([P, P]),
                         ident[:],
                     )
+
+        w_grouped, w_codes, w_scales = {}, {}, {}
 
         def interleave_w(copy, g, h):
             w_grouped[g, h] = work.tile(
@@ -129,7 +142,7 @@ def tile_controlnet_zero_conv_skip_k2_kernel(
             )
             copy(
                 out=w_grouped[g, h][:].rearrange("p (c i) t -> p c t i", i=4),
-                in_=w_raw[g, h].rearrange("p t (c i) -> p c t i", i=4),
+                in_=w_raw[g][:, :, h * GROUP : (h + 1) * GROUP].rearrange("p t (c i) -> p c t i", i=4),
             )
 
         def quantize_w(g, h):
@@ -142,53 +155,54 @@ def tile_controlnet_zero_conv_skip_k2_kernel(
             )
 
         z, base, scaled, y, y_sorted, y_grouped = {}, {}, {}, {}, {}, {}
-        y_codes = keep.tile([P, HALVES, M], U32, name="y_codes", align_bytes=ALIGN)
-        y_scales = keep.tile([P, M], U8, name="y_scales", align_bytes=ALIGN)
 
         def multiply_pass(unit, g):
             i, h = divmod(unit, HALVES)
-            n = 0 if i < SCALE_LOADS[0][1] else 1
-            m0 = (i - SCALE_LOADS[n][0]) * P
             if g == 0:
                 z[unit] = psum.tile([P, GROUP], F32, name="z_%d" % unit, tag="z", bufs=4)
             nc.tensor.matmul_mx(
                 out=z[unit][:],
                 lhsT=c_words[i][:, g, :].bitcast(E5M2X4),
-                lhsT_scale=c_scales[n][:, g, m0 : m0 + P],
+                lhsT_scale=c_scales[i][:, g, :],
                 rhs=w_codes[g, h][:].bitcast(E4M3X4),
                 rhs_scale=w_scales[g, h][:],
                 start=(g == 0),
                 stop=(g == PASSES - 1),
             )
 
-        def multiply(unit):
-            for g in range(PASSES):
-                multiply_pass(unit, g)
+        def multiply(i):
+            for h in range(HALVES):
+                for g in range(PASSES):
+                    multiply_pass(HALVES * i + h, g)
 
         def make_base(unit):
             i, h = divmod(unit, HALVES)
-            base[unit] = work.tile([P, GROUP], F32, name="base_%d" % unit, tag="base", bufs=3)
+            made = work.tile([P, GROUP], F32, name="base_%d" % unit, tag="base", bufs=4)
+            base[unit] = made[:]
             nc.vector.scalar_tensor_tensor(
-                out=base[unit][:], in0=bias_bank[h][:], scalar=vec_cols[:, i : i + 1],
-                in1=skip_sb[i][:, h * GROUP : (h + 1) * GROUP], op0=MULT, op1=ADD,
+                out=base[unit], in0=bias_bank[h][:], scalar=vec_cols[:, i : i + 1],
+                in1=skip_rows[i][:, h * GROUP : (h + 1) * GROUP], op0=MULT, op1=ADD,
             )
 
         def scale_bias(i):
-            scaled[i] = work.tile([P, GROUP], F32, name="scaled_%d" % i, tag="scaled", bufs=2)
-            nc.scalar.activation(out=scaled[i][:], in_=bias_bank[1][:], func=COPY, scale=vec_cols[:, i : i + 1])
+            pair, a = divmod(i, 2)
+            if a == 0:
+                scaled[pair] = work.tile([P, 2, GROUP], F32, name="scaled_%d" % pair, tag="scaled", bufs=3)
+            nc.scalar.activation(out=scaled[pair][:, a, :], in_=bias_high[:], func=COPY, scale=vec_cols[:, i : i + 1])
 
-        def add_skip(i):
-            unit = HALVES * i + 1
-            base[unit] = work.tile([P, GROUP], F32, name="base_%d" % unit, tag="summed", bufs=2)
-            nc.gpsimd.tensor_tensor(out=base[unit][:], in0=scaled[i][:], in1=skip_sb[i][:, GROUP:N], op=ADD)
+        def add_skip(pair):
+            summed = work.tile([P, 2, GROUP], F32, name="summed_%d" % pair, tag="summed", bufs=2)
+            nc.gpsimd.tensor_tensor(out=summed[:], in0=scaled[pair][:], in1=skip_pair[pair][:, :, GROUP:N], op=ADD)
+            for a in range(2):
+                base[HALVES * (2 * pair + a) + 1] = summed[:, a, :]
 
         def finish(unit):
             i, h = divmod(unit, HALVES)
             if h == 0:
-                y[i] = work.tile([P, N], F32, name="y_%d" % i, tag="y", bufs=10, align_bytes=ALIGN)
+                y[i] = work.tile([P, N], F32, name="y_%d" % i, tag="y", bufs=9, align_bytes=ALIGN)
             nc.vector.scalar_tensor_tensor(
                 out=y[i][:, h * GROUP : (h + 1) * GROUP], in0=z[unit][:], scalar=vec_cols[:, i : i + 1],
-                in1=base[unit][:], op0=MULT, op1=ADD,
+                in1=base[unit], op0=MULT, op1=ADD,
             )
 
         def round_sorted(copy, unit):
@@ -200,45 +214,56 @@ def tile_controlnet_zero_conv_skip_k2_kernel(
             )
 
         def turn(i, h0, h1):
-            turned = psum.tile([P, h1 - h0, 2, P], F32, name="turned_%d_%d" % (i, h0), tag="turned", bufs=2)
+            turned = psum.tile([P, h1 - h0, 2, P], F32, name="turned_%d_%d" % (i, h0), tag="turned", bufs=3)
             for h in range(h0, h1):
-                words = y_sorted[HALVES * i + h][:].rearrange("m u p e -> m (u p e)").bitcast(F32)
+                pairs = y_sorted[HALVES * i + h][:].rearrange("m u p e -> m (u p e)").bitcast(F32)
                 for u in range(2):
-                    nc.tensor.transpose(turned[:, h - h0, u, :], words[:, u * P : (u + 1) * P], ident[:])
+                    nc.tensor.transpose(turned[:, h - h0, u, :], pairs[:, u * P : (u + 1) * P], ident[:])
             pair, a = divmod(i, 2)
-            if a == 0 and h0 == 0:
+            if a == 0:
                 y_grouped[pair] = work.tile(
-                    [P, HALVES, 2 * P * PACK], BF16, name="y_grouped_%d" % pair, tag="y_grouped", bufs=3,
+                    [P, HALVES * 2 * P * PACK], BF16, name="y_grouped_%d" % pair, tag="y_grouped", bufs=3,
                     align_bytes=ALIGN,
                 )
-            words_out = y_grouped[pair][:].bitcast(F32).rearrange("p h (m u) -> p h m u", u=2)
-            nc.scalar.copy(
-                out=words_out[:, h0:h1, a * P : (a + 1) * P, :], in_=turned[:].rearrange("p h u m -> p h m u")
-            )
+            grouped = y_grouped[pair][:].bitcast(F32).rearrange("p (h m u) -> p h m u", h=HALVES, u=2)
+            return grouped[:, h0:h1, a * P : (a + 1) * P, :], turned[:].rearrange("p h u m -> p h m u")
+
+        y_words = {
+            (i0, i1): keep.tile([P, HALVES, (i1 - i0) * P], U32, name="y_words_%d" % i0, align_bytes=ALIGN)
+            for i0, i1 in WORD_STORES
+        }
+        y_planes = {
+            (i0, i1): keep.tile([P, HALVES, (i1 - i0) * P], U8, name="y_planes_%d" % i0, align_bytes=ALIGN)
+            for i0, i1 in SCALE_STORES
+        }
+
+        def columns_of(tiles, pair, h):
+            i0, i1 = [span for span in tiles if span[0] <= 2 * pair < span[1]][0]
+            return tiles[i0, i1][:, h, (2 * pair - i0) * P : (2 * pair + 2 - i0) * P]
 
         def quantize_y(pair, h):
-            cols = slice(2 * P * pair, 2 * P * (pair + 1))
+            width = 2 * P * PACK
             nc.vector.quantize_mx(
-                out=y_codes[:, h, cols].bitcast(E4M3X4), scales=y_scales[4 * h : P, cols], in_=y_grouped[pair][:, h, :]
+                out=columns_of(y_words, pair, h).bitcast(E4M3X4),
+                scales=columns_of(y_planes, pair, h),
+                in_=y_grouped[pair][:, h * width : (h + 1) * width],
             )
 
         def store_y(i):
             nc.sync.dma_start(out=out_0[i * P : (i + 1) * P, :], in_=y[i][:])
 
-        def store_planes(tiles_done):
+        def store_planes(pair):
             for i0, i1 in WORD_STORES:
-                if i1 == tiles_done:
+                if i1 == 2 * pair + 2:
                     dst = out_1.rearrange("h p m t -> p h (m t)")[:, :, PACK * i0 * P : PACK * i1 * P]
-                    nc.sync.dma_start(out=dst.bitcast(I32), in_=y_codes[:, :, i0 * P : i1 * P].bitcast(I32))
+                    nc.sync.dma_start(out=dst.bitcast(I32), in_=y_words[i0, i1][:].bitcast(I32))
             for i0, i1 in SCALE_STORES:
-                if i1 == tiles_done:
-                    for q in range(4):
-                        nc.sync.dma_start(
-                            out=out_2[:, 4 * q : 4 * q + 4, i0 * P : i1 * P].bitcast(I32),
-                            in_=y_scales[32 * q : 32 * q + 4 * HALVES, i0 * P : i1 * P].bitcast(I32),
-                        )
+                if i1 == 2 * pair + 2:
+                    for r in range(4):
+                        dst = out_2[:, r:SCALE_ROWS:4, i0 * P : i1 * P].rearrange("h q m -> q h m")
+                        src = y_planes[i0, i1][r:P:QUADRANT, :, :]
+                        nc.sync.dma_start(out=dst.bitcast(I32), in_=src.bitcast(I32))
 
-        first_units = range(2 * HALVES)
         interleave_w(nc.vector.tensor_copy, 0, 0)
         interleave_w(nc.scalar.copy, 0, 1)
         spread_vectors()
@@ -246,52 +271,86 @@ def tile_controlnet_zero_conv_skip_k2_kernel(
         interleave_w(nc.vector.tensor_copy, 1, 0)
         interleave_w(nc.scalar.copy, 1, 1)
         quantize_w(0, 1)
-        for unit in first_units:
-            multiply_pass(unit, 0)
         for h in range(HALVES):
-            quantize_w(1, h)
-            for unit in first_units[h::HALVES]:
-                multiply_pass(unit, 1)
+            multiply_pass(h, 0)
+        quantize_w(1, 0)
         interleave_w(nc.vector.tensor_copy, 2, 0)
         interleave_w(nc.scalar.copy, 2, 1)
-        make_base(0)
+        nc.scalar.copy(out=bias_high[:], in_=bias_bank[1][:])
+        for i in range(2, SCALE_AHEAD + 1):
+            scale_bias(i)
+        quantize_w(1, 1)
         for h in range(HALVES):
-            quantize_w(2, h)
-            for unit in first_units[h::HALVES]:
-                multiply_pass(unit, 2)
+            multiply_pass(h, 1)
+        quantize_w(2, 0)
+        make_base(0)
+        quantize_w(2, 1)
+        for h in range(HALVES):
+            multiply_pass(h, 2)
+        multiply(1)
+
         make_base(1)
-        scale_bias(1)
         add_skip(1)
+        finish(0)
+        round_sorted(nc.scalar.copy, 0)
+        make_base(2)
+        finish(1)
+        store_y(0)
+        multiply(2)
+        make_base(3)
+        round_sorted(nc.scalar.copy, 1)
+        scale_bias(1 + SCALE_AHEAD)
+        finish(2)
+        round_sorted(nc.scalar.copy, 2)
+        make_base(4)
+        finish(3)
+        store_y(1)
 
         last = TILES - 1
-        for i in range(TILES):
-            if 0 < i < last:
-                multiply(2 * i + 2)
-                multiply(2 * i + 3)
-            if 0 < i < last:
-                add_skip(i + 1)
-            if i > 0:
-                round_sorted(nc.scalar.copy, 2 * i - 1)
-            if i + 2 < TILES:
-                scale_bias(i + 2)
+        second_copy = None
+        for i in range(2, last):
+            pair, a = divmod(i, 2)
+            scalar_scales = i + SCALE_AHEAD < TILES
+            vector_copies = scalar_scales and i % VECTOR_COPY_EVERY == 1
+            multiply(i + 1)
+            if a == 0 and pair + 1 < PAIRS:
+                add_skip(pair + 1)
+            if a == 1 and not vector_copies:
+                nc.scalar.copy(*second_copy)
+            round_sorted(nc.scalar.copy, 2 * i - 1)
+            if scalar_scales:
+                scale_bias(i + SCALE_AHEAD)
             finish(2 * i)
             round_sorted(nc.scalar.copy, 2 * i)
-            if i > 0:
-                turn(i - 1, 0, HALVES)
-            if i < last:
-                make_base(2 * i + 2)
-            if i >= 3:
-                pair, h = divmod(i - 3, 2)
-                quantize_y(pair, h)
-                if h == 1:
-                    store_planes(2 * pair + 2)
+            if vector_copies:
+                nc.vector.tensor_copy(*second_copy)
+            if a == 0:
+                first_copy = turn(i - 2, 0, HALVES)
+                second_copy = turn(i - 1, 0, HALVES)
+                nc.scalar.copy(*first_copy)
+            make_base(2 * i + 2)
+            if a == 1 and pair >= QUANTIZE_BEHIND:
+                for h in range(HALVES):
+                    quantize_y(pair - QUANTIZE_BEHIND, h)
+                store_planes(pair - QUANTIZE_BEHIND)
             finish(2 * i + 1)
             store_y(i)
-        pair = TILES // 2 - 1
-        quantize_y(pair - 1, 1)
-        store_planes(TILES - 2)
-        round_sorted(nc.vector.tensor_copy, UNITS - 1)
+
+        round_sorted(nc.scalar.copy, 2 * last - 1)
+        nc.scalar.copy(*second_copy)
         for h in range(HALVES):
-            turn(last, h, h + 1)
-            quantize_y(pair, h)
-        store_planes(TILES)
+            quantize_y(PAIRS - 3, h)
+            finish(2 * last + h)
+        store_y(last)
+        store_planes(PAIRS - 3)
+        nc.scalar.copy(*turn(last - 1, 0, HALVES))
+        for h in range(HALVES):
+            round_sorted(nc.vector.tensor_copy, 2 * last + h)
+        for h in range(HALVES):
+            quantize_y(PAIRS - 2, h)
+        store_planes(PAIRS - 2)
+        nc.scalar.copy(*turn(last, 0, 1))
+        nc.vector.tensor_copy(*turn(last, 1, HALVES))
+        for h in range(HALVES):
+            quantize_y(PAIRS - 1, h)
+        store_planes(PAIRS - 1)

from contextlib import ExitStack

import concourse.mybir as mybir
from concourse.masks import make_identity

M, K, N = 2048, 1536, 1024
FLOPS = 2 * M * K * N

F32 = mybir.dt.float32
BF16 = mybir.dt.bfloat16
I32 = mybir.dt.int32
U32 = mybir.dt.uint32
U8 = mybir.dt.uint8
E4M3X4 = mybir.dt.float8_e4m3fn_x4
E5M2X4 = mybir.dt.float8_e5m2_x4
MULT = mybir.AluOpType.mult
ADD = mybir.AluOpType.add
COPY = mybir.ActivationFunctionType.Copy

P = 128
PACK = 4
GROUP = P * PACK
PASSES = K // GROUP
HALVES = N // GROUP
TILES = M // P
PAIRS = TILES // 2
QUADRANT = 32
SCALE_ROWS = 16
VEC_ROWS = TILES + N // P
ALIGN = 256

WORD_LOADS = [(0, 1), (1, 4), (4, 8), (8, 16)]
SCALE_LOADS = [(0, 4), (4, 16)]
SKIP_LOADS = [(0, 1), (1, 2), (2, 4), (4, 6), (6, 8), (8, 12), (12, 16)]
WORD_STORES = [(0, 6), (6, 10), (10, 12), (12, 14), (14, 16)]
SCALE_STORES = [(0, 8), (8, 16)]

SCALE_AHEAD = 4
QUANTIZE_BEHIND = 2
VECTOR_COPY_EVERY = 4


def tile_controlnet_zero_conv_skip_k2_kernel(
    tc, control_words, control_scales, zero_weight, zero_bias, strength, skip, out_0, out_1, out_2
):
    nc = tc.nc
    with ExitStack() as ctx:
        keep = ctx.enter_context(tc.tile_pool(name="keep", bufs=1))
        work = ctx.enter_context(tc.tile_pool(name="work", bufs=1))
        psum = ctx.enter_context(tc.psum_pool(name="psum", bufs=1))
        ctx.enter_context(tc.manual_schedule())

        ident = keep.tile([P, P], F32, name="ident")
        make_identity(nc, ident[:])

        c_planes = [
            keep.tile([P, PASSES, (i1 - i0) * P], U8, name="c_planes_%d" % i0, align_bytes=ALIGN)
            for i0, i1 in SCALE_LOADS
        ]
        vec_rows = keep.tile([P, P], BF16, name="vec_rows")
        vec_wide = keep.tile([P, P], F32, name="vec_wide")
        vec_cols = keep.tile([P, VEC_ROWS], F32, name="vec_cols")
        nc.vector.memset(vec_wide[:], 0.0)
        for plane in c_planes:
            nc.vector.memset(plane[:].bitcast(I32), 0)

        w_raw, c_words, c_scales, skip_rows, skip_pair = {}, {}, {}, {}, {}

        def load_w(g):
            w_raw[g] = keep.tile([P, PACK, N], BF16, name="w_raw_%d" % g, align_bytes=ALIGN)
            rows = zero_weight[g * GROUP : (g + 1) * GROUP, :]
            nc.sync.dma_start(out=w_raw[g][:], in_=rows.rearrange("(p t) n -> p t n", t=PACK))

        def load_skip(n):
            i0, i1 = SKIP_LOADS[n]
            rows = keep.tile([P, i1 - i0, N], BF16, name="skip_%d" % i0, align_bytes=ALIGN)
            nc.sync.dma_start(out=rows[:], in_=skip[i0 * P : i1 * P, :].rearrange("(a p) n -> p a n", p=P))
            for i in range(i0, i1):
                skip_rows[i] = rows[:, i - i0, :]
                if i % 2 == 0 and i + 1 < i1:
                    skip_pair[i // 2] = rows[:, i - i0 : i - i0 + 2, :]

        def load_words(n):
            i0, i1 = WORD_LOADS[n]
            words = keep.tile([P, PASSES, (i1 - i0) * P], U32, name="c_words_%d" % i0, align_bytes=ALIGN)
            src = control_words.rearrange("g p m t -> p g (m t)")[:, :, PACK * i0 * P : PACK * i1 * P]
            nc.sync.dma_start(out=words[:].bitcast(I32), in_=src.bitcast(I32))
            for i in range(i0, i1):
                c_words[i] = words[:, :, (i - i0) * P : (i - i0 + 1) * P]

        def load_scales(n):
            i0, i1 = SCALE_LOADS[n]
            for r in range(4):
                src = control_scales[:, r:SCALE_ROWS:4, i0 * P : i1 * P].rearrange("g q m -> q g m")
                nc.sync.dma_start(out=c_planes[n][r:P:QUADRANT, :, :].bitcast(I32), in_=src.bitcast(I32))
            for i in range(i0, i1):
                c_scales[i] = c_planes[n][:, :, (i - i0) * P : (i - i0 + 1) * P]

        load_w(0)
        nc.sync.dma_start(out=vec_rows[0:TILES, :], in_=strength.rearrange("(i p) -> i p", p=P))
        nc.sync.dma_start(out=vec_rows[TILES:VEC_ROWS, :], in_=zero_bias.rearrange("(j p) -> j p", p=P))
        load_w(1)
        load_w(2)
        load_scales(0)
        load_words(0)
        load_skip(0)
        load_words(1)
        load_skip(1)
        load_skip(2)
        load_scales(1)
        load_skip(3)
        load_words(2)
        load_skip(4)
        load_words(3)
        load_skip(5)
        load_skip(6)

        bias_bank = {}
        bias_high = keep.tile([P, GROUP], F32, name="bias_high")

        def spread_vectors():
            nc.vector.tensor_copy(out=vec_wide[0:VEC_ROWS, :], in_=vec_rows[0:VEC_ROWS, :])
            vec_turned = psum.tile([P, P], F32, name="vec_turned", tag="turned", bufs=3)
            nc.tensor.transpose(vec_turned[:], vec_wide[:], ident[:])
            nc.scalar.copy(out=vec_cols[:], in_=vec_turned[:, 0:VEC_ROWS])
            bias_bank[0] = psum.tile([P, GROUP], F32, name="bias_0")
            bias_bank[1] = psum.tile([P, GROUP], F32, name="bias_1", tag="turned", bufs=3)
            for h in range(HALVES):
                for j in range(GROUP // P):
                    col = TILES + h * GROUP // P + j
                    nc.tensor.transpose(
                        bias_bank[h][:, j * P : (j + 1) * P],
                        vec_cols[:, col : col + 1].to_broadcast([P, P]),
                        ident[:],
                    )

        w_grouped, w_codes, w_scales = {}, {}, {}

        def interleave_w(copy, g, h):
            w_grouped[g, h] = work.tile(
                [P, GROUP, PACK], BF16, name="w_grouped_%d_%d" % (g, h), tag="w_grouped", bufs=4, align_bytes=ALIGN
            )
            copy(
                out=w_grouped[g, h][:].rearrange("p (c i) t -> p c t i", i=4),
                in_=w_raw[g][:, :, h * GROUP : (h + 1) * GROUP].rearrange("p t (c i) -> p c t i", i=4),
            )

        def quantize_w(g, h):
            w_codes[g, h] = keep.tile([P, GROUP], U32, name="w_codes_%d_%d" % (g, h), align_bytes=ALIGN)
            w_scales[g, h] = keep.tile([P, GROUP], U8, name="w_scales_%d_%d" % (g, h), align_bytes=ALIGN)
            nc.vector.quantize_mx(
                out=w_codes[g, h][:].bitcast(E4M3X4),
                scales=w_scales[g, h][:],
                in_=w_grouped[g, h][:].rearrange("p n t -> p (n t)"),
            )

        z, base, scaled, y, y_sorted, y_grouped = {}, {}, {}, {}, {}, {}

        def multiply_pass(unit, g):
            i, h = divmod(unit, HALVES)
            if g == 0:
                z[unit] = psum.tile([P, GROUP], F32, name="z_%d" % unit, tag="z", bufs=4)
            nc.tensor.matmul_mx(
                out=z[unit][:],
                lhsT=c_words[i][:, g, :].bitcast(E5M2X4),
                lhsT_scale=c_scales[i][:, g, :],
                rhs=w_codes[g, h][:].bitcast(E4M3X4),
                rhs_scale=w_scales[g, h][:],
                start=(g == 0),
                stop=(g == PASSES - 1),
            )

        def multiply(i):
            for h in range(HALVES):
                for g in range(PASSES):
                    multiply_pass(HALVES * i + h, g)

        def make_base(unit):
            i, h = divmod(unit, HALVES)
            made = work.tile([P, GROUP], F32, name="base_%d" % unit, tag="base", bufs=4)
            base[unit] = made[:]
            nc.vector.scalar_tensor_tensor(
                out=base[unit], in0=bias_bank[h][:], scalar=vec_cols[:, i : i + 1],
                in1=skip_rows[i][:, h * GROUP : (h + 1) * GROUP], op0=MULT, op1=ADD,
            )

        def scale_bias(i):
            pair, a = divmod(i, 2)
            if a == 0:
                scaled[pair] = work.tile([P, 2, GROUP], F32, name="scaled_%d" % pair, tag="scaled", bufs=3)
            nc.scalar.activation(out=scaled[pair][:, a, :], in_=bias_high[:], func=COPY, scale=vec_cols[:, i : i + 1])

        def add_skip(pair):
            summed = work.tile([P, 2, GROUP], F32, name="summed_%d" % pair, tag="summed", bufs=2)
            nc.gpsimd.tensor_tensor(out=summed[:], in0=scaled[pair][:], in1=skip_pair[pair][:, :, GROUP:N], op=ADD)
            for a in range(2):
                base[HALVES * (2 * pair + a) + 1] = summed[:, a, :]

        def finish(unit):
            i, h = divmod(unit, HALVES)
            if h == 0:
                y[i] = work.tile([P, N], F32, name="y_%d" % i, tag="y", bufs=9, align_bytes=ALIGN)
            nc.vector.scalar_tensor_tensor(
                out=y[i][:, h * GROUP : (h + 1) * GROUP], in0=z[unit][:], scalar=vec_cols[:, i : i + 1],
                in1=base[unit], op0=MULT, op1=ADD,
            )

        def round_sorted(copy, unit):
            i, h = divmod(unit, HALVES)
            y_sorted[unit] = work.tile([P, 2, P, 2], BF16, name="y_sorted_%d" % unit, tag="y_sorted", bufs=6)
            copy(
                out=y_sorted[unit][:],
                in_=y[i][:, h * GROUP : (h + 1) * GROUP].rearrange("m (p u e) -> m u p e", u=2, e=2),
            )

        def turn(i, h0, h1):
            turned = psum.tile([P, h1 - h0, 2, P], F32, name="turned_%d_%d" % (i, h0), tag="turned", bufs=3)
            for h in range(h0, h1):
                pairs = y_sorted[HALVES * i + h][:].rearrange("m u p e -> m (u p e)").bitcast(F32)
                for u in range(2):
                    nc.tensor.transpose(turned[:, h - h0, u, :], pairs[:, u * P : (u + 1) * P], ident[:])
            pair, a = divmod(i, 2)
            if a == 0:
                y_grouped[pair] = work.tile(
                    [P, HALVES * 2 * P * PACK], BF16, name="y_grouped_%d" % pair, tag="y_grouped", bufs=3,
                    align_bytes=ALIGN,
                )
            grouped = y_grouped[pair][:].bitcast(F32).rearrange("p (h m u) -> p h m u", h=HALVES, u=2)
            return grouped[:, h0:h1, a * P : (a + 1) * P, :], turned[:].rearrange("p h u m -> p h m u")

        y_words = {
            (i0, i1): keep.tile([P, HALVES, (i1 - i0) * P], U32, name="y_words_%d" % i0, align_bytes=ALIGN)
            for i0, i1 in WORD_STORES
        }
        y_planes = {
            (i0, i1): keep.tile([P, HALVES, (i1 - i0) * P], U8, name="y_planes_%d" % i0, align_bytes=ALIGN)
            for i0, i1 in SCALE_STORES
        }

        def columns_of(tiles, pair, h):
            i0, i1 = [span for span in tiles if span[0] <= 2 * pair < span[1]][0]
            return tiles[i0, i1][:, h, (2 * pair - i0) * P : (2 * pair + 2 - i0) * P]

        def quantize_y(pair, h):
            width = 2 * P * PACK
            nc.vector.quantize_mx(
                out=columns_of(y_words, pair, h).bitcast(E4M3X4),
                scales=columns_of(y_planes, pair, h),
                in_=y_grouped[pair][:, h * width : (h + 1) * width],
            )

        def store_y(i):
            nc.sync.dma_start(out=out_0[i * P : (i + 1) * P, :], in_=y[i][:])

        def store_planes(pair):
            for i0, i1 in WORD_STORES:
                if i1 == 2 * pair + 2:
                    dst = out_1.rearrange("h p m t -> p h (m t)")[:, :, PACK * i0 * P : PACK * i1 * P]
                    nc.sync.dma_start(out=dst.bitcast(I32), in_=y_words[i0, i1][:].bitcast(I32))
            for i0, i1 in SCALE_STORES:
                if i1 == 2 * pair + 2:
                    for r in range(4):
                        dst = out_2[:, r:SCALE_ROWS:4, i0 * P : i1 * P].rearrange("h q m -> q h m")
                        src = y_planes[i0, i1][r:P:QUADRANT, :, :]
                        nc.sync.dma_start(out=dst.bitcast(I32), in_=src.bitcast(I32))

        interleave_w(nc.vector.tensor_copy, 0, 0)
        interleave_w(nc.scalar.copy, 0, 1)
        spread_vectors()
        quantize_w(0, 0)
        interleave_w(nc.vector.tensor_copy, 1, 0)
        interleave_w(nc.scalar.copy, 1, 1)
        quantize_w(0, 1)
        for h in range(HALVES):
            multiply_pass(h, 0)
        quantize_w(1, 0)
        interleave_w(nc.vector.tensor_copy, 2, 0)
        interleave_w(nc.scalar.copy, 2, 1)
        nc.scalar.copy(out=bias_high[:], in_=bias_bank[1][:])
        for i in range(2, SCALE_AHEAD + 1):
            scale_bias(i)
        quantize_w(1, 1)
        for h in range(HALVES):
            multiply_pass(h, 1)
        quantize_w(2, 0)
        make_base(0)
        quantize_w(2, 1)
        for h in range(HALVES):
            multiply_pass(h, 2)
        multiply(1)

        make_base(1)
        add_skip(1)
        finish(0)
        round_sorted(nc.scalar.copy, 0)
        make_base(2)
        finish(1)
        store_y(0)
        multiply(2)
        make_base(3)
        round_sorted(nc.scalar.copy, 1)
        scale_bias(1 + SCALE_AHEAD)
        finish(2)
        round_sorted(nc.scalar.copy, 2)
        make_base(4)
        finish(3)
        store_y(1)

        last = TILES - 1
        second_copy = None
        for i in range(2, last):
            pair, a = divmod(i, 2)
            scalar_scales = i + SCALE_AHEAD < TILES
            vector_copies = scalar_scales and i % VECTOR_COPY_EVERY == 1
            multiply(i + 1)
            if a == 0 and pair + 1 < PAIRS:
                add_skip(pair + 1)
            if a == 1 and not vector_copies:
                nc.scalar.copy(*second_copy)
            round_sorted(nc.scalar.copy, 2 * i - 1)
            if scalar_scales:
                scale_bias(i + SCALE_AHEAD)
            finish(2 * i)
            round_sorted(nc.scalar.copy, 2 * i)
            if vector_copies:
                nc.vector.tensor_copy(*second_copy)
            if a == 0:
                first_copy = turn(i - 2, 0, HALVES)
                second_copy = turn(i - 1, 0, HALVES)
                nc.scalar.copy(*first_copy)
            make_base(2 * i + 2)
            if a == 1 and pair >= QUANTIZE_BEHIND:
                for h in range(HALVES):
                    quantize_y(pair - QUANTIZE_BEHIND, h)
                store_planes(pair - QUANTIZE_BEHIND)
            finish(2 * i + 1)
            store_y(i)

        round_sorted(nc.scalar.copy, 2 * last - 1)
        nc.scalar.copy(*second_copy)
        for h in range(HALVES):
            quantize_y(PAIRS - 3, h)
            finish(2 * last + h)
        store_y(last)
        store_planes(PAIRS - 3)
        nc.scalar.copy(*turn(last - 1, 0, HALVES))
        for h in range(HALVES):
            round_sorted(nc.vector.tensor_copy, 2 * last + h)
        for h in range(HALVES):
            quantize_y(PAIRS - 2, h)
        store_planes(PAIRS - 2)
        nc.scalar.copy(*turn(last, 0, 1))
        nc.vector.tensor_copy(*turn(last, 1, HALVES))
        for h in range(HALVES):
            quantize_y(PAIRS - 1, h)
        store_planes(PAIRS - 1)
